import numpy as np
import ml_dtypes


def mxq(x, axis, fmt="e4m3"):
    dtype, down = {"e4m3": (ml_dtypes.float8_e4m3fn, 7), "e5m2": (ml_dtypes.float8_e5m2, 14)}[fmt]
    v = np.moveaxis(np.asarray(x, np.float32).astype(ml_dtypes.bfloat16).astype(np.float64), axis, -1)
    blocks = v.reshape(v.shape[:-1] + (-1, 32))
    amax = np.abs(blocks).max(-1, keepdims=True)
    byte = np.maximum(np.where(amax > 0, np.frexp(amax)[1] - 1 + 127, 0) - down, 1)
    scale = np.exp2(byte - 127.0)
    codes = (blocks / scale).astype(np.float32).astype(dtype).astype(np.float64)
    return np.moveaxis((codes * scale).reshape(v.shape), -1, axis)


WIDE = False


def mx_kscale(k):
    if not WIDE:
        return np.ones(k)
    levels = np.array([10, -10, 5, -5, 0])
    if k % 512:
        return np.exp2(np.random.permutation(np.resize(levels, k // 32))).repeat(32)
    a = np.empty((k // 512, 16))
    for p in range(k // 512):
        a[p, :8] = np.random.permutation(np.resize(levels, 8))
        for g in range(8):
            far = levels[np.abs(levels - a[p, g]) >= 10]
            a[p, g + 8] = far[np.random.randint(len(far))]
    return np.exp2(a.ravel()).repeat(32)


def f64(x):
    return np.asarray(x).astype(np.float64)


def striped(idx):
    return np.tile(idx.reshape(-1, 16).T, (8, 1)).astype(np.uint16)


def unstriped(offs):
    return offs[:16].T.reshape(-1).astype(np.int64)


def pack_weight(w):
    k, n = w.shape
    w = f64(np.asarray(w, np.float32).astype(ml_dtypes.bfloat16)).reshape(k // 32, 32, n)
    amax = np.abs(w).max(1)
    byte = np.clip(np.where(amax > 0, np.frexp(amax)[1] - 1 + 127 - 7, 1), 1, 254)
    scaled = (w * np.exp2(127.0 - byte)[:, None, :]).reshape(k, n).astype(np.float32)
    words = np.ascontiguousarray(scaled.reshape(k // 512, 128, 4, n).transpose(0, 1, 3, 2)).astype(ml_dtypes.float8_e4m3fn).view(np.uint8)
    return words, np.ascontiguousarray(byte.astype(np.uint8).reshape(k // 512, 16, n))


def unpack_weight(words, scales):
    g, p, n, _ = words.shape
    vals = np.ascontiguousarray(words).view(ml_dtypes.float8_e4m3fn).astype(np.float64) * np.repeat(np.exp2(scales.astype(np.float64) - 127.0), 8, axis=1)[..., None]
    return vals.transpose(0, 1, 3, 2).reshape(g * 512, n)


K, T, S, N, D = 1024, 1024, 512, 128, 3
P = 2 ** 7


def setup_inputs():
    n = np.random.standard_normal
    s = mx_kscale(K)[:, None]
    packed_xT = pack_weight(n((K, T)) * s)
    return {
        "x_words": packed_xT[0],
        "x_scales": packed_xT[1],
        "w1": (n((K, N)) / np.sqrt(K) / s).astype(np.float32),
        "coup": (np.tile(np.random.uniform(-0.8, 0.8, (D, 1, S)), (1, P, 1))).astype(np.float32),
        "field": (0.5 * n((N, S))).astype(np.float32),
        "offs": striped(np.random.permutation(T)[:S]),
        "pos1": striped(np.random.permutation(S)[:S]),
        "pos2": striped(np.random.permutation(S)[:S]),
        "pos3": striped(np.random.permutation(S)[:S]),
    }


def reference(x_words, x_scales, w1, coup, field, offs, pos1, pos2, pos3):
    xq = unpack_weight(x_words, x_scales)[:, unstriped(offs)]
    y = mxq(f64(w1), 0, "e4m3").T @ xq
    mag = np.tanh(y)
    chi = -1.0 * ((mag) ** 2) + 1.0
    loc = f64(field) + mag[:, unstriped(pos1)] * f64(coup)[0, :1] + mag[:, unstriped(pos2)] * f64(coup)[1, :1] + mag[:, unstriped(pos3)] * f64(coup)[2, :1] - (mag * ((chi[:, unstriped(pos1)] * f64(coup)[0, :1]) * f64(coup)[0, :1] + (chi[:, unstriped(pos2)] * f64(coup)[1, :1]) * f64(coup)[1, :1] + (chi[:, unstriped(pos3)] * f64(coup)[2, :1]) * f64(coup)[2, :1]))
    mnew = 0.6 * np.tanh(loc) + 0.4 * mag
    return mnew * (f64(field) + 0.5 * (mnew[:, unstriped(pos1)] * f64(coup)[0, :1] + mnew[:, unstriped(pos2)] * f64(coup)[1, :1] + mnew[:, unstriped(pos3)] * f64(coup)[2, :1])) - (0.5 * (np.log(-1.0 * ((mnew) ** 2) + 1.05)))

@@ -1,0 +1,234 @@
+from contextlib import ExitStack
+
+import concourse.mybir as mybir
+from concourse.masks import make_identity
+
+K, T, S, N, D = 1024, 1024, 512, 128, 3
+FLOPS = 2 * K * N * S
+
+F32 = mybir.dt.float32
+BF16 = mybir.dt.bfloat16
+I32 = mybir.dt.int32
+U32 = mybir.dt.uint32
+U16 = mybir.dt.uint16
+U8 = mybir.dt.uint8
+FP8X4 = mybir.dt.float8_e4m3fn_x4
+ACT = mybir.ActivationFunctionType
+ALU = mybir.AluOpType
+
+P = 128
+PACK = 4
+PASSES = K // (P * PACK)
+HALF = S // 2
+LANES = 16
+
+
+def tile_picked_ytapm_en_p_kernel(
+    tc, x_words, x_scales, w1, coup, field, offs, pos1, pos2, pos3, out
+):
+    nc = tc.nc
+    with ExitStack() as ctx:
+        sb = ctx.enter_context(tc.tile_pool(name="sb", bufs=1))
+        ps = ctx.enter_context(tc.psum_pool(name="ps", bufs=1))
+
+        def f32(name, width=S):
+            return sb.tile([P, width], F32, name=name)
+
+        halves = [slice(h * HALF, (h + 1) * HALF) for h in range(2)]
+        lcols = [slice(h * HALF // LANES, (h + 1) * HALF // LANES) for h in range(2)]
+
+        pick = sb.tile([P, S // LANES], U16, name="pick")
+        nc.sync.dma_start(pick[:], offs)
+        xs = sb.tile([P, T], U8, name="xs")
+        nc.gpsimd.memset(xs[:].bitcast(I32), 0)
+        warm = f32("warm", 8)
+        nc.vector.memset(warm[:], 0.0)
+        for q in range(4):
+            nc.scalar.dma_start(
+                xs[32 * q : 32 * q + 4 * PASSES, :].bitcast(I32),
+                x_scales[:, 4 * q : 4 * q + 4, :].bitcast(I32),
+            )
+        warm2 = f32("warm2", 8)
+        nc.scalar.activation(warm2[:], warm[:], ACT.Sigmoid)
+        xw = [sb.tile([P, T], I32, name="xw%d" % g) for g in range(PASSES)]
+        wraw = [sb.tile([P, PACK, N], F32, name="wraw%d" % g) for g in range(PASSES)]
+        ccol = sb.tile([P, D, PACK], F32, name="ccol")
+        nc.sync.dma_start(ccol[:], coup[:, 0, :].rearrange("d (p k) -> p d k", k=PACK))
+        nc.sync.dma_start(xw[0][:], x_words[0].rearrange("p n t -> p (n t)").bitcast(I32))
+        nc.sync.dma_start(wraw[0][:], w1[0:512, :].rearrange("(p j) n -> p j n", j=PACK))
+        nc.sync.dma_start(xw[1][:], x_words[1].rearrange("p n t -> p (n t)").bitcast(I32))
+        nc.sync.dma_start(wraw[1][:], w1[512:1024, :].rearrange("(p j) n -> p j n", j=PACK))
+        pos = []
+        for d, src in enumerate((pos1, pos2, pos3)):
+            lst = sb.tile([P, S // LANES], U16, name="pos%d" % d)
+            nc.sync.dma_start(lst[:], src)
+            pos.append(lst)
+        fld = f32("fld")
+        cpl = [f32("cpl%d" % d) for d in range(D)]
+        nc.sync.dma_start(cpl[0][:], coup[0])
+        nc.sync.dma_start(cpl[1][:], coup[1])
+        nc.sync.dma_start(fld[:], field)
+        nc.sync.dma_start(cpl[2][:], coup[2])
+
+        ident = sb.tile([P, P], F32, name="ident")
+        make_identity(nc, ident[:])
+        csqcol = sb.tile([P, D, PACK], F32, name="csqcol")
+        sq01 = sb.tile([P, PACK], F32, name="sq01")
+        sqsum = sb.tile([P, PACK], F32, name="sqsum")
+        nc.gpsimd.tensor_tensor(csqcol[:], ccol[:], ccol[:], ALU.mult)
+        nc.gpsimd.tensor_tensor(sq01[:], csqcol[:, 0, :], csqcol[:, 1, :], ALU.add)
+        nc.gpsimd.tensor_tensor(sqsum[:], sq01[:], csqcol[:, 2, :], ALU.add)
+        csq = ps.tile([P, S], F32, name="csq")
+        for k in range(PACK):
+            nc.tensor.transpose(csq[:, k::PACK], sqsum[:, k : k + 1].to_broadcast([P, P]), ident[:])
+
+        gw = [sb.tile([P, S], U32, name="gw%d" % g, align_bytes=64) for g in range(PASSES)]
+        gs = sb.tile([P, S], U8, name="gs", align_bytes=64)
+        wbf = [sb.tile([P, N, PACK], BF16, name="wbf%d" % g, align_bytes=64) for g in range(PASSES)]
+        wq = [sb.tile([P, N], U32, name="wq%d" % g, align_bytes=64) for g in range(PASSES)]
+        wsc = [sb.tile([P, N], U8, name="wsc%d" % g, align_bytes=64) for g in range(PASSES)]
+        for g in range(PASSES):
+            nc.gpsimd.memset(wsc[g][:], 0)
+
+        def quantize(g):
+            nc.vector.quantize_mx(
+                out=wq[g][:].bitcast(FP8X4),
+                scales=wsc[g][:],
+                in_=wbf[g][:].rearrange("p n j -> p (n j)"),
+            )
+
+        for g in range(PASSES):
+            nc.scalar.copy(wbf[g][:], wraw[g][:].rearrange("p j n -> p n j"))
+        nc.vector.tensor_copy(gs[:], xs[:].indirect(pick[:]))
+        nc.vector.tensor_copy(gw[0][:], xw[0][:].bitcast(U32).indirect(pick[:]))
+        quantize(0)
+        nc.vector.tensor_copy(gw[1][:, halves[0]], xw[1][:].bitcast(U32).indirect(pick[:, lcols[0]]))
+        quantize(1)
+        nc.vector.tensor_copy(gw[1][:, halves[1]], xw[1][:].bitcast(U32).indirect(pick[:, lcols[1]]))
+
+        ybank = [ps.tile([P, HALF], F32, name="ybank%d" % h) for h in range(2)]
+        for h in range(2):
+            for g in range(PASSES):
+                nc.tensor.matmul_mx(
+                    out=ybank[h][:],
+                    lhsT=wq[g][:].bitcast(FP8X4),
+                    lhsT_scale=wsc[g][:],
+                    rhs=gw[g][:, halves[h]].bitcast(FP8X4),
+                    rhs_scale=gs[4 * g : P, halves[h]],
+                    start=(g == 0),
+                    stop=(g == PASSES - 1),
+                )
+        y = f32("y")
+        nc.scalar.copy(y[:, halves[0]], ybank[0][:])
+        nc.vector.tensor_copy(y[:, halves[1]], ybank[1][:])
+
+        fld8 = f32("fld8")
+        nc.scalar.activation(fld8[:], fld[:], ACT.Copy, scale=0.8)
+
+        sig = [f32("sig%d" % d) for d in range(D)]
+        g_ = [f32("g%d" % d) for d in range(D)]
+        gsq = [f32("gsq%d" % d) for d in range(D)]
+        acc_a = [f32("acca%d" % d) for d in range(D)]
+        acc_b = [f32("accb%d" % d) for d in range(D)]
+        mag, react, loc, th, mnew = (f32(n) for n in ("mag", "react", "loc", "th", "mnew"))
+        base = f32("base")
+
+        def gather_sig(dst, window, d, h):
+            nc.scalar.activation(
+                dst[:, halves[h]], window[:].indirect(pos[d][:, lcols[h]]), ACT.Sigmoid, scale=2.0
+            )
+
+        def couple(dst, src, d, h):
+            c = halves[h]
+            nc.vector.scalar_tensor_tensor(
+                dst[:, c], src[:, c], -0.5, cpl[d][:, c], ALU.add, ALU.mult
+            )
+
+        def add_a(d, h):
+            c = halves[h]
+            prev = fld if d == 0 else acc_a[d - 1]
+            nc.vector.scalar_tensor_tensor(acc_a[d][:, c], g_[d][:, c], 2.0, prev[:, c], ALU.mult, ALU.add)
+
+        def sub_b(d, h):
+            c = halves[h]
+            prev = csq if d == 0 else acc_b[d - 1]
+            nc.vector.tensor_tensor(acc_b[d][:, c], prev[:, c], gsq[d][:, c], ALU.subtract)
+
+        def square(d, h):
+            c = halves[h]
+            nc.scalar.activation(gsq[d][:, c], g_[d][:, c], ACT.Square, scale=2.0)
+
+        def mix(h):
+            c = halves[h]
+            nc.vector.scalar_tensor_tensor(mnew[:, c], th[:, c], 1.5, mag[:, c], ALU.mult, ALU.add)
+
+        def make_base(h):
+            c = halves[h]
+            nc.vector.scalar_tensor_tensor(
+                base[:, c], acc_a[D - 1][:, c], 0.2, fld8[:, c], ALU.mult, ALU.add
+            )
+
+        for h in range(2):
+            c = halves[h]
+            gather_sig(sig[0], y, 0, h)
+            gather_sig(sig[1], y, 1, h)
+            couple(g_[0], sig[0], 0, h)
+            square(0, h)
+            gather_sig(sig[2], y, 2, h)
+            couple(g_[1], sig[1], 1, h)
+            add_a(0, h)
+            square(1, h)
+            sub_b(0, h)
+            add_a(1, h)
+            couple(g_[2], sig[2], 2, h)
+            square(2, h)
+            nc.scalar.activation(mag[:, c], y[:, c], ACT.Tanh)
+            sub_b(1, h)
+            add_a(2, h)
+            sub_b(2, h)
+            if h == 1:
+                make_base(0)
+            nc.vector.tensor_tensor(react[:, c], mag[:, c], acc_b[D - 1][:, c], ALU.mult)
+            if h == 1:
+                mix(0)
+            nc.vector.tensor_tensor(loc[:, c], acc_a[D - 1][:, c], react[:, c], ALU.subtract)
+            nc.scalar.activation(th[:, c], loc[:, c], ACT.Tanh)
+        make_base(1)
+        mix(1)
+
+        sig2 = [f32("sigc%d" % d) for d in range(D)]
+        hh = [f32("h%d" % d) for d in range(D)]
+        acc_z = [f32("accz%d" % d) for d in range(D)]
+        msq, prod, res = (f32(n) for n in ("msq", "prod", "res"))
+
+        def add_z(d, h):
+            c = halves[h]
+            prev = base if d == 0 else acc_z[d - 1]
+            nc.vector.scalar_tensor_tensor(acc_z[d][:, c], hh[d][:, c], 0.3 if d == 0 else 0.6, prev[:, c], ALU.mult, ALU.add)
+
+        for h in range(2):
+            for d in (1, 2):
+                gather_sig(sig2[d], loc, d, h)
+        for h in range(2):
+            c = halves[h]
+            nc.vector.tensor_tensor(hh[0][:, c], th[:].indirect(pos[0][:, lcols[h]]), cpl[0][:, c], ALU.mult)
+        for h in range(2):
+            couple(hh[1], sig2[1], 1, h)
+            add_z(0, h)
+            couple(hh[2], sig2[2], 2, h)
+            add_z(1, h)
+        for h in range(2):
+            add_z(2, h)
+        for h in range(2):
+            c = halves[h]
+            nc.scalar.activation(msq[:, c], mnew[:, c], ACT.Square, scale=0.4)
+        for h in range(2):
+            c = halves[h]
+            nc.scalar.activation(loc[:, c], msq[:, c], ACT.Ln, scale=-1.0, bias=1.05)
+            nc.vector.scalar_tensor_tensor(
+                prod[:, c], mnew[:, c], 0.4, acc_z[D - 1][:, c], ALU.mult, ALU.mult
+            )
+        for h in range(2):
+            c = halves[h]
+            nc.vector.scalar_tensor_tensor(res[:, c], loc[:, c], -0.5, prod[:, c], ALU.mult, ALU.add)
+            nc.sync.dma_start(out[:, c], res[:, c])

@@ -40,97 +40,94 @@ def tile_picked_ytapm_en_p_kernel(
         pick = sb.tile([P, S // LANES], U16, name="pick")
         nc.sync.dma_start(pick[:], offs)
         xs = sb.tile([P, T], U8, name="xs")
-        nc.gpsimd.memset(xs[:].bitcast(I32), 0)
-        warm = f32("warm", 8)
-        nc.vector.memset(warm[:], 0.0)
-        for q in range(4):
-            nc.scalar.dma_start(
+        nc.vector.memset(xs[:].bitcast(I32), 0)
+        def load_scales(queue, q):
+            queue.dma_start(
                 xs[32 * q : 32 * q + 4 * PASSES, :].bitcast(I32),
                 x_scales[:, 4 * q : 4 * q + 4, :].bitcast(I32),
             )
-        warm2 = f32("warm2", 8)
-        nc.scalar.activation(warm2[:], warm[:], ACT.Sigmoid)
+
+        load_scales(nc.scalar, 2)
+        load_scales(nc.scalar, 3)
+        warm = f32("warm", 16)
+        nc.vector.memset(warm[:, 0:8], 0.0)
+        nc.scalar.activation(warm[:, 8:16], warm[:, 0:8], ACT.Sigmoid)
         xw = [sb.tile([P, T], I32, name="xw%d" % g) for g in range(PASSES)]
         wraw = [sb.tile([P, PACK, N], F32, name="wraw%d" % g) for g in range(PASSES)]
         ccol = sb.tile([P, D, PACK], F32, name="ccol")
-        nc.sync.dma_start(ccol[:], coup[:, 0, :].rearrange("d (p k) -> p d k", k=PACK))
-        nc.sync.dma_start(xw[0][:], x_words[0].rearrange("p n t -> p (n t)").bitcast(I32))
         nc.sync.dma_start(wraw[0][:], w1[0:512, :].rearrange("(p j) n -> p j n", j=PACK))
-        nc.sync.dma_start(xw[1][:], x_words[1].rearrange("p n t -> p (n t)").bitcast(I32))
+        load_scales(nc.sync, 0)
+        load_scales(nc.sync, 1)
         nc.sync.dma_start(wraw[1][:], w1[512:1024, :].rearrange("(p j) n -> p j n", j=PACK))
-        pos = []
-        for d, src in enumerate((pos1, pos2, pos3)):
-            lst = sb.tile([P, S // LANES], U16, name="pos%d" % d)
-            nc.sync.dma_start(lst[:], src)
-            pos.append(lst)
-        fld = f32("fld")
+        nc.sync.dma_start(xw[0][:], x_words[0].rearrange("p n t -> p (n t)").bitcast(I32))
+        nc.sync.dma_start(xw[1][:], x_words[1].rearrange("p n t -> p (n t)").bitcast(I32))
+        pos = [sb.tile([P, S // LANES], U16, name="pos%d" % d) for d in range(D)]
         cpl = [f32("cpl%d" % d) for d in range(D)]
+        fld = f32("fld")
+        nc.sync.dma_start(ccol[:], coup[:, 0, :].rearrange("d (p k) -> p d k", k=PACK))
+        for lst, src in zip(pos, (pos1, pos2, pos3)):
+            nc.sync.dma_start(lst[:], src)
         nc.sync.dma_start(cpl[0][:], coup[0])
-        nc.sync.dma_start(cpl[1][:], coup[1])
         nc.sync.dma_start(fld[:], field)
+        nc.sync.dma_start(cpl[1][:], coup[1])
         nc.sync.dma_start(cpl[2][:], coup[2])
 
         ident = sb.tile([P, P], F32, name="ident")
         make_identity(nc, ident[:])
-        csqcol = sb.tile([P, D, PACK], F32, name="csqcol")
-        sq01 = sb.tile([P, PACK], F32, name="sq01")
-        sqsum = sb.tile([P, PACK], F32, name="sqsum")
-        nc.gpsimd.tensor_tensor(csqcol[:], ccol[:], ccol[:], ALU.mult)
-        nc.gpsimd.tensor_tensor(sq01[:], csqcol[:, 0, :], csqcol[:, 1, :], ALU.add)
-        nc.gpsimd.tensor_tensor(sqsum[:], sq01[:], csqcol[:, 2, :], ALU.add)
-        csq = ps.tile([P, S], F32, name="csq")
-        for k in range(PACK):
-            nc.tensor.transpose(csq[:, k::PACK], sqsum[:, k : k + 1].to_broadcast([P, P]), ident[:])
 
-        gw = [sb.tile([P, S], U32, name="gw%d" % g, align_bytes=64) for g in range(PASSES)]
         gs = sb.tile([P, S], U8, name="gs", align_bytes=64)
-        wbf = [sb.tile([P, N, PACK], BF16, name="wbf%d" % g, align_bytes=64) for g in range(PASSES)]
-        wq = [sb.tile([P, N], U32, name="wq%d" % g, align_bytes=64) for g in range(PASSES)]
-        wsc = [sb.tile([P, N], U8, name="wsc%d" % g, align_bytes=64) for g in range(PASSES)]
+        wbf = sb.tile([P, PASSES, N, PACK], BF16, name="wbf", tag="staged", align_bytes=64)
+        wq = sb.tile([P, PASSES, N], U32, name="wq", align_bytes=64)
+        wsc = sb.tile([P, PASSES, N], U8, name="wsc", align_bytes=64)
         for g in range(PASSES):
-            nc.gpsimd.memset(wsc[g][:], 0)
-
-        def quantize(g):
-            nc.vector.quantize_mx(
-                out=wq[g][:].bitcast(FP8X4),
-                scales=wsc[g][:],
-                in_=wbf[g][:].rearrange("p n j -> p (n j)"),
-            )
-
-        for g in range(PASSES):
-            nc.scalar.copy(wbf[g][:], wraw[g][:].rearrange("p j n -> p n j"))
+            nc.scalar.copy(wbf[:, g], wraw[g][:].rearrange("p j n -> p n j"))
         nc.vector.tensor_copy(gs[:], xs[:].indirect(pick[:]))
+        nc.vector.quantize_mx(
+            out=wq[:].rearrange("p g n -> p (g n)").bitcast(FP8X4),
+            scales=wsc[:].rearrange("p g n -> p (g n)"),
+            in_=wbf[:].rearrange("p g n j -> p (g n j)"),
+        )
+        gw = [
+            sb.tile([P, S], U32, name="gw0", tag="staged", align_bytes=64),
+            sb.tile([P, S], U32, name="gw1", align_bytes=64),
+        ]
+        pieces = [(0, 256), (256, 384), (384, 512)]
         nc.vector.tensor_copy(gw[0][:], xw[0][:].bitcast(U32).indirect(pick[:]))
-        quantize(0)
-        nc.vector.tensor_copy(gw[1][:, halves[0]], xw[1][:].bitcast(U32).indirect(pick[:, lcols[0]]))
-        quantize(1)
-        nc.vector.tensor_copy(gw[1][:, halves[1]], xw[1][:].bitcast(U32).indirect(pick[:, lcols[1]]))
+        for a, b in pieces:
+            nc.vector.tensor_copy(gw[1][:, a:b], xw[1][:].bitcast(U32).indirect(pick[:, a // LANES : b // LANES]))
 
-        ybank = [ps.tile([P, HALF], F32, name="ybank%d" % h) for h in range(2)]
-        for h in range(2):
-            for g in range(PASSES):
+        ybank = [ps.tile([P, b - a], F32, name="ybank%d" % a) for a, b in pieces]
+        for g in range(PASSES):
+            for bank, (a, b) in zip(ybank, pieces):
                 nc.tensor.matmul_mx(
-                    out=ybank[h][:],
-                    lhsT=wq[g][:].bitcast(FP8X4),
-                    lhsT_scale=wsc[g][:],
-                    rhs=gw[g][:, halves[h]].bitcast(FP8X4),
-                    rhs_scale=gs[4 * g : P, halves[h]],
+                    out=bank[:],
+                    lhsT=wq[:, g, :].bitcast(FP8X4),
+                    lhsT_scale=wsc[:, g, :],
+                    rhs=gw[g][:, a:b].bitcast(FP8X4),
+                    rhs_scale=gs[4 * g : P, a:b],
                     start=(g == 0),
                     stop=(g == PASSES - 1),
                 )
         y = f32("y")
-        nc.scalar.copy(y[:, halves[0]], ybank[0][:])
-        nc.vector.tensor_copy(y[:, halves[1]], ybank[1][:])
+        for bank, (a, b) in zip(ybank[:-1], pieces[:-1]):
+            nc.scalar.copy(y[:, a:b], bank[:])
+        nc.vector.tensor_copy(y[:, pieces[-1][0] :], ybank[-1][:])
 
-        fld8 = f32("fld8")
-        nc.scalar.activation(fld8[:], fld[:], ACT.Copy, scale=0.8)
+        csqcol = sb.tile([P, D, PACK], F32, name="csqcol")
+        sqsum = sb.tile([P, PACK], F32, name="sqsum")
+        csq = ps.tile([P, S], F32, name="csq")
+        nc.vector.tensor_tensor(csqcol[:], ccol[:], ccol[:], ALU.mult)
+        nc.vector.tensor_reduce(sqsum[:], csqcol[:].rearrange("p d k -> p k d"), mybir.AxisListType.X, ALU.add)
+        for k in range(PACK):
+            nc.tensor.transpose(csq[:, k::PACK], sqsum[:, k : k + 1].to_broadcast([P, P]), ident[:])
 
         sig = [f32("sig%d" % d) for d in range(D)]
         g_ = [f32("g%d" % d) for d in range(D)]
         gsq = [f32("gsq%d" % d) for d in range(D)]
         acc_a = [f32("acca%d" % d) for d in range(D)]
         acc_b = [f32("accb%d" % d) for d in range(D)]
-        mag, react, loc, th, mnew = (f32(n) for n in ("mag", "react", "loc", "th", "mnew"))
+        react, loc, th, mnew = (f32(n) for n in ("react", "loc", "th", "mnew"))
+        mag = g_[D - 1]
         base = f32("base")
 
         def gather_sig(dst, window, d, h):
@@ -154,10 +151,6 @@ def tile_picked_ytapm_en_p_kernel(
             prev = csq if d == 0 else acc_b[d - 1]
             nc.vector.tensor_tensor(acc_b[d][:, c], prev[:, c], gsq[d][:, c], ALU.subtract)
 
-        def square(d, h):
-            c = halves[h]
-            nc.scalar.activation(gsq[d][:, c], g_[d][:, c], ACT.Square, scale=2.0)
-
         def mix(h):
             c = halves[h]
             nc.vector.scalar_tensor_tensor(mnew[:, c], th[:, c], 1.5, mag[:, c], ALU.mult, ALU.add)
@@ -165,36 +158,32 @@ def tile_picked_ytapm_en_p_kernel(
         def make_base(h):
             c = halves[h]
             nc.vector.scalar_tensor_tensor(
-                base[:, c], acc_a[D - 1][:, c], 0.2, fld8[:, c], ALU.mult, ALU.add
+                base[:, c], acc_a[D - 1][:, c], 0.25, fld[:, c], ALU.mult, ALU.add
             )
 
-        for h in range(2):
-            c = halves[h]
-            gather_sig(sig[0], y, 0, h)
-            gather_sig(sig[1], y, 1, h)
-            couple(g_[0], sig[0], 0, h)
-            square(0, h)
-            gather_sig(sig[2], y, 2, h)
-            couple(g_[1], sig[1], 1, h)
-            add_a(0, h)
-            square(1, h)
-            sub_b(0, h)
-            add_a(1, h)
-            couple(g_[2], sig[2], 2, h)
-            square(2, h)
-            nc.scalar.activation(mag[:, c], y[:, c], ACT.Tanh)
-            sub_b(1, h)
-            add_a(2, h)
-            sub_b(2, h)
-            if h == 1:
-                make_base(0)
+        steps = [(d, h) for d in range(D) for h in range(2)]
+        for d, h in steps:
+            gather_sig(sig[d], y, d, h)
+        for i, (d, h) in enumerate(steps):
+            couple(g_[d], sig[d], d, h)
+            if i > 0:
+                add_a(*steps[i - 1])
+        for d in range(D):
+            nc.scalar.activation(gsq[d][:], g_[d][:], ACT.Square, scale=2.0)
+        sub_b(*steps[0])
+        add_a(*steps[-1])
+        nc.scalar.activation(mag[:], y[:], ACT.Tanh)
+        for d, h in steps[1:]:
+            sub_b(d, h)
+        for c in halves:
             nc.vector.tensor_tensor(react[:, c], mag[:, c], acc_b[D - 1][:, c], ALU.mult)
-            if h == 1:
-                mix(0)
+        for c in halves:
             nc.vector.tensor_tensor(loc[:, c], acc_a[D - 1][:, c], react[:, c], ALU.subtract)
             nc.scalar.activation(th[:, c], loc[:, c], ACT.Tanh)
-        make_base(1)
-        mix(1)
+        for h in range(2):
+            make_base(h)
+        for h in range(2):
+            mix(h)
 
         sig2 = [f32("sigc%d" % d) for d in range(D)]
         hh = [f32("h%d" % d) for d in range(D)]
@@ -204,29 +193,26 @@ def tile_picked_ytapm_en_p_kernel(
         def add_z(d, h):
             c = halves[h]
             prev = base if d == 0 else acc_z[d - 1]
-            nc.vector.scalar_tensor_tensor(acc_z[d][:, c], hh[d][:, c], 0.3 if d == 0 else 0.6, prev[:, c], ALU.mult, ALU.add)
+            nc.vector.scalar_tensor_tensor(acc_z[d][:, c], hh[d][:, c], 0.375 if d == 0 else 0.75, prev[:, c], ALU.mult, ALU.add)
 
-        for h in range(2):
-            for d in (1, 2):
+        for d in (1, 2):
+            for h in range(2):
                 gather_sig(sig2[d], loc, d, h)
         for h in range(2):
             c = halves[h]
             nc.vector.tensor_tensor(hh[0][:, c], th[:].indirect(pos[0][:, lcols[h]]), cpl[0][:, c], ALU.mult)
-        for h in range(2):
-            couple(hh[1], sig2[1], 1, h)
-            add_z(0, h)
-            couple(hh[2], sig2[2], 2, h)
-            add_z(1, h)
-        for h in range(2):
-            add_z(2, h)
-        for h in range(2):
-            c = halves[h]
-            nc.scalar.activation(msq[:, c], mnew[:, c], ACT.Square, scale=0.4)
+        for d in range(D):
+            for h in range(2):
+                if d > 0:
+                    couple(hh[d], sig2[d], d, h)
+            for h in range(2):
+                add_z(d, h)
+        nc.scalar.activation(msq[:], mnew[:], ACT.Square, scale=0.4)
         for h in range(2):
             c = halves[h]
             nc.scalar.activation(loc[:, c], msq[:, c], ACT.Ln, scale=-1.0, bias=1.05)
             nc.vector.scalar_tensor_tensor(
-                prod[:, c], mnew[:, c], 0.4, acc_z[D - 1][:, c], ALU.mult, ALU.mult
+                prod[:, c], mnew[:, c], 0.32, acc_z[D - 1][:, c], ALU.mult, ALU.mult
             )
         for h in range(2):
             c = halves[h]

@@ -109,9 +109,12 @@ def tile_picked_ytapm_en_p_kernel(
                     stop=(g == PASSES - 1),
                 )
         y = f32("y")
-        for bank, (a, b) in zip(ybank[:-1], pieces[:-1]):
-            nc.scalar.copy(y[:, a:b], bank[:])
-        nc.vector.tensor_copy(y[:, pieces[-1][0] :], ybank[-1][:])
+        mag = f32("mag")
+        for bank, (a, b) in zip(ybank[1:], pieces[1:]):
+            nc.scalar.activation(mag[:, a:b], bank[:], ACT.Tanh)
+        for bank, (a, b) in zip(ybank, pieces):
+            nc.vector.tensor_copy(y[:, a:b], bank[:])
+        nc.scalar.activation(mag[:, halves[0]], ybank[0][:], ACT.Tanh)
 
         csqcol = sb.tile([P, D, PACK], F32, name="csqcol")
         sqsum = sb.tile([P, PACK], F32, name="sqsum")
@@ -125,9 +128,8 @@ def tile_picked_ytapm_en_p_kernel(
         g_ = [f32("g%d" % d) for d in range(D)]
         gsq = [f32("gsq%d" % d) for d in range(D)]
         acc_a = [f32("acca%d" % d) for d in range(D)]
-        acc_b = [f32("accb%d" % d) for d in range(D)]
+        acc_b = [sig[D - 1]] + [f32("accb%d" % d) for d in range(1, D)]
         react, loc, th, mnew = (f32(n) for n in ("react", "loc", "th", "mnew"))
-        mag = g_[D - 1]
         base = f32("base")
 
         def gather_sig(dst, window, d, h):
@@ -144,7 +146,7 @@ def tile_picked_ytapm_en_p_kernel(
         def add_a(d, h):
             c = halves[h]
             prev = fld if d == 0 else acc_a[d - 1]
-            nc.vector.scalar_tensor_tensor(acc_a[d][:, c], g_[d][:, c], 2.0, prev[:, c], ALU.mult, ALU.add)
+            nc.vector.scalar_tensor_tensor(acc_a[d][:, c], g_[d][:, c], 1.0 if (d, h) == (0, 0) else 2.0, prev[:, c], ALU.mult, ALU.add)
 
         def sub_b(d, h):
             c = halves[h]
@@ -162,19 +164,23 @@ def tile_picked_ytapm_en_p_kernel(
             )
 
         steps = [(d, h) for d in range(D) for h in range(2)]
-        for d, h in steps:
-            gather_sig(sig[d], y, d, h)
-        for i, (d, h) in enumerate(steps):
-            couple(g_[d], sig[d], d, h)
-            if i > 0:
-                add_a(*steps[i - 1])
-        for d in range(D):
-            nc.scalar.activation(gsq[d][:], g_[d][:], ACT.Square, scale=2.0)
-        sub_b(*steps[0])
-        add_a(*steps[-1])
-        nc.scalar.activation(mag[:], y[:], ACT.Tanh)
         for d, h in steps[1:]:
-            sub_b(d, h)
+            gather_sig(sig[d], y, d, h)
+        c = halves[0]
+        nc.vector.tensor_tensor(g_[0][:, c], mag[:].indirect(pos[0][:, lcols[0]]), cpl[0][:, c], ALU.mult)
+        for d in range(D):
+            for h in range(2):
+                if (d, h) != (0, 0):
+                    couple(g_[d], sig[d], d, h)
+            for h in range(2):
+                add_a(d, h)
+        nc.scalar.activation(gsq[0][:, halves[0]], g_[0][:, halves[0]], ACT.Square)
+        nc.scalar.activation(gsq[0][:, halves[1]], g_[0][:, halves[1]], ACT.Square, scale=2.0)
+        for d in range(1, D):
+            nc.scalar.activation(gsq[d][:], g_[d][:], ACT.Square, scale=2.0)
+        for d in range(D):
+            for h in range(2):
+                sub_b(d, h)
         for c in halves:
             nc.vector.tensor_tensor(react[:, c], mag[:, c], acc_b[D - 1][:, c], ALU.mult)
         for c in halves:

from contextlib import ExitStack

import concourse.mybir as mybir
from concourse.masks import make_identity

K, T, S, N, D = 1024, 1024, 512, 128, 3
FLOPS = 2 * K * N * S

F32 = mybir.dt.float32
BF16 = mybir.dt.bfloat16
I32 = mybir.dt.int32
U32 = mybir.dt.uint32
U16 = mybir.dt.uint16
U8 = mybir.dt.uint8
FP8X4 = mybir.dt.float8_e4m3fn_x4
ACT = mybir.ActivationFunctionType
ALU = mybir.AluOpType

P = 128
PACK = 4
PASSES = K // (P * PACK)
HALF = S // 2
LANES = 16


def tile_picked_ytapm_en_p_kernel(
    tc, x_words, x_scales, w1, coup, field, offs, pos1, pos2, pos3, out
):
    nc = tc.nc
    with ExitStack() as ctx:
        sb = ctx.enter_context(tc.tile_pool(name="sb", bufs=1))
        ps = ctx.enter_context(tc.psum_pool(name="ps", bufs=1))

        def f32(name, width=S):
            return sb.tile([P, width], F32, name=name)

        halves = [slice(h * HALF, (h + 1) * HALF) for h in range(2)]
        lcols = [slice(h * HALF // LANES, (h + 1) * HALF // LANES) for h in range(2)]

        pick = sb.tile([P, S // LANES], U16, name="pick")
        nc.sync.dma_start(pick[:], offs)
        xs = sb.tile([P, T], U8, name="xs")
        nc.vector.memset(xs[:].bitcast(I32), 0)
        def load_scales(queue, q):
            queue.dma_start(
                xs[32 * q : 32 * q + 4 * PASSES, :].bitcast(I32),
                x_scales[:, 4 * q : 4 * q + 4, :].bitcast(I32),
            )

        load_scales(nc.scalar, 2)
        load_scales(nc.scalar, 3)
        warm = f32("warm", 16)
        nc.vector.memset(warm[:, 0:8], 0.0)
        nc.scalar.activation(warm[:, 8:16], warm[:, 0:8], ACT.Sigmoid)
        xw = [sb.tile([P, T], I32, name="xw%d" % g) for g in range(PASSES)]
        wraw = [sb.tile([P, PACK, N], F32, name="wraw%d" % g) for g in range(PASSES)]
        ccol = sb.tile([P, D, PACK], F32, name="ccol")
        nc.sync.dma_start(wraw[0][:], w1[0:512, :].rearrange("(p j) n -> p j n", j=PACK))
        load_scales(nc.sync, 0)
        load_scales(nc.sync, 1)
        nc.sync.dma_start(wraw[1][:], w1[512:1024, :].rearrange("(p j) n -> p j n", j=PACK))
        nc.sync.dma_start(xw[0][:], x_words[0].rearrange("p n t -> p (n t)").bitcast(I32))
        nc.sync.dma_start(xw[1][:], x_words[1].rearrange("p n t -> p (n t)").bitcast(I32))
        pos = [sb.tile([P, S // LANES], U16, name="pos%d" % d) for d in range(D)]
        cpl = [f32("cpl%d" % d) for d in range(D)]
        fld = f32("fld")
        nc.sync.dma_start(ccol[:], coup[:, 0, :].rearrange("d (p k) -> p d k", k=PACK))
        for lst, src in zip(pos, (pos1, pos2, pos3)):
            nc.sync.dma_start(lst[:], src)
        nc.sync.dma_start(cpl[0][:], coup[0])
        nc.sync.dma_start(fld[:], field)
        nc.sync.dma_start(cpl[1][:], coup[1])
        nc.sync.dma_start(cpl[2][:], coup[2])

        ident = sb.tile([P, P], F32, name="ident")
        make_identity(nc, ident[:])

        gs = sb.tile([P, S], U8, name="gs", align_bytes=64)
        wbf = sb.tile([P, PASSES, N, PACK], BF16, name="wbf", tag="staged", align_bytes=64)
        wq = sb.tile([P, PASSES, N], U32, name="wq", align_bytes=64)
        wsc = sb.tile([P, PASSES, N], U8, name="wsc", align_bytes=64)
        for g in range(PASSES):
            nc.scalar.copy(wbf[:, g], wraw[g][:].rearrange("p j n -> p n j"))
        nc.vector.tensor_copy(gs[:], xs[:].indirect(pick[:]))
        nc.vector.quantize_mx(
            out=wq[:].rearrange("p g n -> p (g n)").bitcast(FP8X4),
            scales=wsc[:].rearrange("p g n -> p (g n)"),
            in_=wbf[:].rearrange("p g n j -> p (g n j)"),
        )
        gw = [
            sb.tile([P, S], U32, name="gw0", tag="staged", align_bytes=64),
            sb.tile([P, S], U32, name="gw1", align_bytes=64),
        ]
        pieces = [(0, 256), (256, 384), (384, 512)]
        nc.vector.tensor_copy(gw[0][:], xw[0][:].bitcast(U32).indirect(pick[:]))
        for a, b in pieces:
            nc.vector.tensor_copy(gw[1][:, a:b], xw[1][:].bitcast(U32).indirect(pick[:, a // LANES : b // LANES]))

        ybank = [ps.tile([P, b - a], F32, name="ybank%d" % a) for a, b in pieces]
        for g in range(PASSES):
            for bank, (a, b) in zip(ybank, pieces):
                nc.tensor.matmul_mx(
                    out=bank[:],
                    lhsT=wq[:, g, :].bitcast(FP8X4),
                    lhsT_scale=wsc[:, g, :],
                    rhs=gw[g][:, a:b].bitcast(FP8X4),
                    rhs_scale=gs[4 * g : P, a:b],
                    start=(g == 0),
                    stop=(g == PASSES - 1),
                )
        y = f32("y")
        mag = f32("mag")
        for bank, (a, b) in zip(ybank[1:], pieces[1:]):
            nc.scalar.activation(mag[:, a:b], bank[:], ACT.Tanh)
        for bank, (a, b) in zip(ybank, pieces):
            nc.vector.tensor_copy(y[:, a:b], bank[:])
        nc.scalar.activation(mag[:, halves[0]], ybank[0][:], ACT.Tanh)

        csqcol = sb.tile([P, D, PACK], F32, name="csqcol")
        sqsum = sb.tile([P, PACK], F32, name="sqsum")
        csq = ps.tile([P, S], F32, name="csq")
        nc.vector.tensor_tensor(csqcol[:], ccol[:], ccol[:], ALU.mult)
        nc.vector.tensor_reduce(sqsum[:], csqcol[:].rearrange("p d k -> p k d"), mybir.AxisListType.X, ALU.add)
        for k in range(PACK):
            nc.tensor.transpose(csq[:, k::PACK], sqsum[:, k : k + 1].to_broadcast([P, P]), ident[:])

        sig = [f32("sig%d" % d) for d in range(D)]
        g_ = [f32("g%d" % d) for d in range(D)]
        gsq = [f32("gsq%d" % d) for d in range(D)]
        acc_a = [f32("acca%d" % d) for d in range(D)]
        acc_b = [sig[D - 1]] + [f32("accb%d" % d) for d in range(1, D)]
        react, loc, th, mnew = (f32(n) for n in ("react", "loc", "th", "mnew"))
        base = f32("base")

        def gather_sig(dst, window, d, h):
            nc.scalar.activation(
                dst[:, halves[h]], window[:].indirect(pos[d][:, lcols[h]]), ACT.Sigmoid, scale=2.0
            )

        def couple(dst, src, d, h):
            c = halves[h]
            nc.vector.scalar_tensor_tensor(
                dst[:, c], src[:, c], -0.5, cpl[d][:, c], ALU.add, ALU.mult
            )

        def add_a(d, h):
            c = halves[h]
            prev = fld if d == 0 else acc_a[d - 1]
            nc.vector.scalar_tensor_tensor(acc_a[d][:, c], g_[d][:, c], 1.0 if (d, h) == (0, 0) else 2.0, prev[:, c], ALU.mult, ALU.add)

        def sub_b(d, h):
            c = halves[h]
            prev = csq if d == 0 else acc_b[d - 1]
            nc.vector.tensor_tensor(acc_b[d][:, c], prev[:, c], gsq[d][:, c], ALU.subtract)

        def mix(h):
            c = halves[h]
            nc.vector.scalar_tensor_tensor(mnew[:, c], th[:, c], 1.5, mag[:, c], ALU.mult, ALU.add)

        def make_base(h):
            c = halves[h]
            nc.vector.scalar_tensor_tensor(
                base[:, c], acc_a[D - 1][:, c], 0.25, fld[:, c], ALU.mult, ALU.add
            )

        steps = [(d, h) for d in range(D) for h in range(2)]
        for d, h in steps[1:]:
            gather_sig(sig[d], y, d, h)
        c = halves[0]
        nc.vector.tensor_tensor(g_[0][:, c], mag[:].indirect(pos[0][:, lcols[0]]), cpl[0][:, c], ALU.mult)
        for d in range(D):
            for h in range(2):
                if (d, h) != (0, 0):
                    couple(g_[d], sig[d], d, h)
            for h in range(2):
                add_a(d, h)
        nc.scalar.activation(gsq[0][:, halves[0]], g_[0][:, halves[0]], ACT.Square)
        nc.scalar.activation(gsq[0][:, halves[1]], g_[0][:, halves[1]], ACT.Square, scale=2.0)
        for d in range(1, D):
            nc.scalar.activation(gsq[d][:], g_[d][:], ACT.Square, scale=2.0)
        for d in range(D):
            for h in range(2):
                sub_b(d, h)
        for c in halves:
            nc.vector.tensor_tensor(react[:, c], mag[:, c], acc_b[D - 1][:, c], ALU.mult)
        for c in halves:
            nc.vector.tensor_tensor(loc[:, c], acc_a[D - 1][:, c], react[:, c], ALU.subtract)
            nc.scalar.activation(th[:, c], loc[:, c], ACT.Tanh)
        for h in range(2):
            make_base(h)
        for h in range(2):
            mix(h)

        sig2 = [f32("sigc%d" % d) for d in range(D)]
        hh = [f32("h%d" % d) for d in range(D)]
        acc_z = [f32("accz%d" % d) for d in range(D)]
        msq, prod, res = (f32(n) for n in ("msq", "prod", "res"))

        def add_z(d, h):
            c = halves[h]
            prev = base if d == 0 else acc_z[d - 1]
            nc.vector.scalar_tensor_tensor(acc_z[d][:, c], hh[d][:, c], 0.375 if d == 0 else 0.75, prev[:, c], ALU.mult, ALU.add)

        for d in (1, 2):
            for h in range(2):
                gather_sig(sig2[d], loc, d, h)
        for h in range(2):
            c = halves[h]
            nc.vector.tensor_tensor(hh[0][:, c], th[:].indirect(pos[0][:, lcols[h]]), cpl[0][:, c], ALU.mult)
        for d in range(D):
            for h in range(2):
                if d > 0:
                    couple(hh[d], sig2[d], d, h)
            for h in range(2):
                add_z(d, h)
        nc.scalar.activation(msq[:], mnew[:], ACT.Square, scale=0.4)
        for h in range(2):
            c = halves[h]
            nc.scalar.activation(loc[:, c], msq[:, c], ACT.Ln, scale=-1.0, bias=1.05)
            nc.vector.scalar_tensor_tensor(
                prod[:, c], mnew[:, c], 0.32, acc_z[D - 1][:, c], ALU.mult, ALU.mult
            )
        for h in range(2):
            c = halves[h]
            nc.vector.scalar_tensor_tensor(res[:, c], loc[:, c], -0.5, prod[:, c], ALU.mult, ALU.add)
            nc.sync.dma_start(out[:, c], res[:, c])
